import numpy as np
import ml_dtypes


def mxq(x, axis, fmt="e4m3"):
    dtype, down = {"e4m3": (ml_dtypes.float8_e4m3fn, 7), "e5m2": (ml_dtypes.float8_e5m2, 14)}[fmt]
    v = np.moveaxis(np.asarray(x, np.float32).astype(ml_dtypes.bfloat16).astype(np.float64), axis, -1)
    blocks = v.reshape(v.shape[:-1] + (-1, 32))
    amax = np.abs(blocks).max(-1, keepdims=True)
    byte = np.maximum(np.where(amax > 0, np.frexp(amax)[1] - 1 + 127, 0) - down, 1)
    scale = np.exp2(byte - 127.0)
    codes = (blocks / scale).astype(np.float32).astype(dtype).astype(np.float64)
    return np.moveaxis((codes * scale).reshape(v.shape), -1, axis)


WIDE = False


def mx_kscale(k):
    if not WIDE:
        return np.ones(k)
    levels = np.array([10, -10, 5, -5, 0])
    if k % 512:
        return np.exp2(np.random.permutation(np.resize(levels, k // 32))).repeat(32)
    a = np.empty((k // 512, 16))
    for p in range(k // 512):
        a[p, :8] = np.random.permutation(np.resize(levels, 8))
        for g in range(8):
            far = levels[np.abs(levels - a[p, g]) >= 10]
            a[p, g + 8] = far[np.random.randint(len(far))]
    return np.exp2(a.ravel()).repeat(32)


def f64(x):
    return np.asarray(x).astype(np.float64)


def striped(idx):
    return np.tile(np.asarray(idx).reshape(-1, 16).T, (8, 1)).astype(np.uint16)


def unstriped(offs):
    return offs[:16].T.reshape(-1).astype(np.int64)


E2M1 = np.array([0.0, 0.5, 1.0, 1.5, 2.0, 3.0, 4.0, 6.0, -0.0, -0.5, -1.0, -1.5, -2.0, -3.0, -4.0, -6.0])


def pack_weight(w, fmt):
    k, n = w.shape
    w = f64(np.asarray(w, np.float32).astype(ml_dtypes.bfloat16)).reshape(k // 32, 32, n)
    amax = np.abs(w).max(1)
    if fmt == "e4m3":
        byte = np.frexp(amax)[1] - 1 + 127 - 7
    else:
        mant, ex = np.frexp(amax / 6.0)
        byte = np.where(mant > 0.5, ex, ex - 1) + 127
    byte = np.clip(np.where(amax > 0, byte, 1), 1, 254)
    scaled = (w * np.exp2(127.0 - byte)[:, None, :]).reshape(k, n).astype(np.float32)
    by_word = np.ascontiguousarray(scaled.reshape(k // 512, 128, 4, n).transpose(0, 1, 3, 2))
    if fmt == "e4m3":
        words = by_word.astype(ml_dtypes.float8_e4m3fn).view(np.uint8)
    else:
        c = by_word.astype(ml_dtypes.float4_e2m1fn).view(np.uint8) & 0xF
        words = (c[..., 0::2] | (c[..., 1::2] << 4)).reshape(k // 512, 128, 2 * n)
    return np.ascontiguousarray(words), np.ascontiguousarray(byte.astype(np.uint8).reshape(k // 512, 16, n))


def unpack_weight(words, scales, fmt):
    g, _, n = scales.shape
    words = np.ascontiguousarray(words).reshape(g, 128, n, -1)
    if fmt == "e4m3":
        vals = words.view(ml_dtypes.float8_e4m3fn).astype(np.float64)
    else:
        nib = np.empty((g, 128, n, 4), np.uint8)
        nib[..., 0::2] = words & 0xF
        nib[..., 1::2] = words >> 4
        vals = E2M1[nib]
    vals = vals * np.repeat(np.exp2(scales.astype(np.float64) - 127.0), 8, axis=1)[..., None]
    return vals.transpose(0, 1, 3, 2).reshape(g * 512, n)


K, T, S, L, J, N = 512, 1024, 1024, 512, 512, 512


def setup_inputs():
    n = np.random.standard_normal
    idx = np.random.permutation(T)[:J]
    idx2 = np.random.permutation(S)[:J]
    fk = mx_kscale(K)
    fl = mx_kscale(L)
    wp = pack_weight(n((K, N)) * 1 / np.sqrt(K) * fk[:, None], "e2m1")
    xqp = pack_weight(n((L, S)) / fl[:, None], "e4m3")
    wqp = pack_weight(n((L, N)) * 1 / np.sqrt(L) * fl[:, None], "e2m1")
    return {
        "xa": (n((K, T))).astype(np.float32),
        "xb": (n((K, S))).astype(np.float32),
        "fk": (np.random.uniform(0.5, 2.0, (K, 1)) / fk[:, None]).astype(np.float32),
        "w_words": wp[0],
        "w_scales": wp[1],
        "xq_words": xqp[0],
        "xq_scales": xqp[1],
        "wq_words": wqp[0],
        "wq_scales": wqp[1],
        "offs": striped(idx),
        "offs2": striped(idx2),
    }


def reference(xa, xb, fk, w_words, w_scales, xq_words, xq_scales, wq_words, wq_scales, offs, offs2):
    idx = unstriped(offs)
    idx2 = unstriped(offs2)
    wu = unpack_weight(w_words, w_scales, "e2m1")
    xqu = unpack_weight(xq_words, xq_scales, "e4m3")
    wqu = unpack_weight(wq_words, wq_scales, "e2m1")
    pr = f64(xa)[:, idx] * f64(xb)[:, idx2] * f64(fk)
    prq = mxq(pr, 0, "e4m3")
    xqidx2g = xqu[:, idx2]
    y = wu.T @ prq + wqu.T @ xqidx2g
    return y

@@ -1,0 +1,175 @@
+from contextlib import ExitStack
+
+import concourse.mybir as mybir
+
+K, T, S, L, J, N = 512, 1024, 1024, 512, 512, 512
+FLOPS = 2 * (K + L) * N * J
+
+F32 = mybir.dt.float32
+BF16 = mybir.dt.bfloat16
+I32 = mybir.dt.int32
+U32 = mybir.dt.uint32
+U16 = mybir.dt.uint16
+U8 = mybir.dt.uint8
+FP8X4 = mybir.dt.float8_e4m3fn_x4
+FP4X4 = mybir.dt.float4_e2m1fn_x4
+MULT = mybir.AluOpType.mult
+COPY = mybir.ActivationFunctionType.Copy
+
+P = 128
+PACK = 4
+CHUNK = 128
+CHUNKS = J // CHUNK
+M_TILE = 128
+HALF = 2
+LIST_COLS = CHUNK // 16
+
+
+def tile_list_products_of_two_tables_kernel(
+    tc, xa, xb, fk, w_words, w_scales, xq_words, xq_scales, wq_words, wq_scales, offs, offs2, out
+):
+    nc = tc.nc
+    last = PACK - 1
+    with ExitStack() as ctx:
+        keep = ctx.enter_context(tc.tile_pool(name="keep", bufs=1))
+        psum = ctx.enter_context(tc.psum_pool(name="psum", bufs=1))
+
+        list_a = keep.tile([P, J // 16], U16, name="list_a")
+        list_b = keep.tile([P, J // 16], U16, name="list_b")
+        a_planes = [keep.tile([P, T], F32, name="a%d" % t) for t in range(PACK)]
+        b_planes = [keep.tile([P, S], F32, name="b%d" % t) for t in range(PACK)]
+        fk_sb = keep.tile([P, PACK], F32, name="fk_sb")
+        xq_table = keep.tile([P, S], I32, name="xq_table", align_bytes=64)
+        xs_table = keep.tile([P, S], U8, name="xs_table", align_bytes=64)
+        w_sb = keep.tile([P, 2 * N], U8, name="w_sb", align_bytes=64)
+        wq_sb = keep.tile([P, 2 * N], U8, name="wq_sb", align_bytes=64)
+        ws_sb = keep.tile([P, N], U8, name="ws_sb", align_bytes=64)
+        wqs_sb = keep.tile([P, N], U8, name="wqs_sb", align_bytes=64)
+
+        nc.gpsimd.memset(xs_table[:].bitcast(I32), 0)
+        nc.gpsimd.memset(ws_sb[:].bitcast(I32), 0)
+        nc.gpsimd.memset(wqs_sb[:].bitcast(I32), 0)
+
+        xa_planes = xa.rearrange("(p t) c -> t p c", t=PACK)
+        xb_planes = xb.rearrange("(p t) c -> t p c", t=PACK)
+
+        def load_scale_rows(queue, plane, scales, q):
+            queue.dma_start(
+                out=plane[32 * q : 32 * q + 4, :].bitcast(I32), in_=scales[0, 4 * q : 4 * q + 4, :].bitcast(I32)
+            )
+
+        def load_a(t):
+            nc.sync.dma_start(out=a_planes[t][:], in_=xa_planes[t])
+
+        def load_b(t):
+            nc.sync.dma_start(out=b_planes[t][:], in_=xb_planes[t])
+
+        nc.sync.dma_start(list_b[:], offs2)
+        load_a(0)
+        nc.sync.dma_start(list_a[:], offs)
+        load_b(0)
+        for q in range(4):
+            load_scale_rows(nc.scalar, xs_table, xq_scales, q)
+        load_a(1)
+        load_b(1)
+        nc.sync.dma_start(out=fk_sb[:], in_=fk.rearrange("(p t) o -> p (t o)", t=PACK))
+        load_a(2)
+        load_b(2)
+        for q in range(3):
+            load_scale_rows(nc.sync, wqs_sb, wq_scales, q)
+        nc.sync.dma_start(out=xq_table[:], in_=xq_words[0].rearrange("p n t -> p (n t)").bitcast(I32))
+        load_scale_rows(nc.sync, wqs_sb, wq_scales, 3)
+        load_scale_rows(nc.sync, ws_sb, w_scales, 0)
+        load_a(3)
+        load_b(3)
+        for q in range(1, 4):
+            load_scale_rows(nc.sync, ws_sb, w_scales, q)
+        nc.sync.dma_start(out=wq_sb[:].bitcast(I32), in_=wq_words[0].bitcast(I32))
+        nc.sync.dma_start(out=w_sb[:].bitcast(I32), in_=w_words[0].bitcast(I32))
+
+        xs_picked = keep.tile([P, J], U8, name="xs_picked", align_bytes=64)
+        nc.vector.tensor_copy(xs_picked[:], xs_table[:].indirect(list_b[:]))
+
+        grouped = [
+            keep.tile([P, CHUNK, PACK], BF16, name="grouped%d" % c, tag="g%d" % c, align_bytes=64)
+            for c in range(CHUNKS)
+        ]
+
+        def scale_round(c, t, prod):
+            nc.scalar.activation(grouped[c][:, :, t], prod, COPY, scale=fk_sb[:, t : t + 1])
+
+        a_picked = []
+        for t in range(PACK):
+            picked = keep.tile([P, J], F32, name="a_picked%d" % t)
+            nc.vector.tensor_copy(picked[:], a_planes[t][:].indirect(list_a[:]))
+            a_picked.append(picked)
+            if t < last:
+                prod = keep.tile([P, J], F32, name="prod%d" % t)
+                nc.vector.tensor_tensor(prod[:], b_planes[t][:].indirect(list_b[:]), picked[:], MULT)
+                for c in range(CHUNKS):
+                    scale_round(c, t, prod[:, c * CHUNK : (c + 1) * CHUNK])
+
+        def chunk_list(c):
+            return list_b[:, c * LIST_COLS : (c + 1) * LIST_COLS]
+
+        def last_product(c, tag):
+            prod = keep.tile([P, CHUNK], F32, name="prod_last%d" % c, tag=tag, align_bytes=64)
+            nc.vector.tensor_tensor(
+                prod[:], b_planes[last][:].indirect(chunk_list(c)), a_picked[last][:, c * CHUNK : (c + 1) * CHUNK], MULT
+            )
+            scale_round(c, last, prod[:])
+
+        banks = {}
+
+        def passes(c, words, scales, rhs, rhs_scale, first):
+            for h in range(HALF):
+                if first:
+                    banks[c, h] = psum.tile([P, HALF * CHUNK], F32, name="bank%d_%d" % (c, h))
+                for i in range(HALF):
+                    m = HALF * h + i
+                    nc.tensor.matmul_mx(
+                        out=banks[c, h][:, i * CHUNK : (i + 1) * CHUNK],
+                        lhsT=words[:, 2 * m * M_TILE : 2 * (m + 1) * M_TILE].bitcast(FP4X4),
+                        lhsT_scale=scales[:, m * M_TILE : (m + 1) * M_TILE],
+                        rhs=rhs.bitcast(FP8X4),
+                        rhs_scale=rhs_scale,
+                        start=(first and i == 0),
+                        stop=(not first and i == HALF - 1),
+                    )
+
+        def pick_words(c, tag):
+            picked = keep.tile([P, CHUNK], U32, name="xq_picked%d" % c, tag=tag, align_bytes=64)
+            nc.vector.tensor_copy(picked[:], xq_table[:].bitcast(U32).indirect(chunk_list(c)))
+            passes(c, wq_sb, wqs_sb, picked[:], xs_picked[:, c * CHUNK : (c + 1) * CHUNK], True)
+
+        out_v = out.rearrange("(h i p) j -> h p i j", h=HALF, i=HALF)
+
+        def finish(c):
+            codes = keep.tile([P, CHUNK], U32, name="codes%d" % c, align_bytes=64)
+            scales = keep.tile([P, CHUNK], U8, name="scales%d" % c, align_bytes=64)
+            nc.vector.quantize_mx(
+                out=codes[:].bitcast(FP8X4), scales=scales[:], in_=grouped[c][:].rearrange("p j t -> p (j t)")
+            )
+            passes(c, w_sb, ws_sb, codes[:], scales[:], False)
+
+        def store(c):
+            for h in range(HALF):
+                staged = keep.tile([P, HALF, CHUNK], F32, name="staged%d_%d" % (c, h))
+                flat = staged[:].rearrange("p i j -> p (i j)")
+                if c == CHUNKS - 1 and h == 1:
+                    nc.vector.tensor_copy(flat, banks[c, h][:])
+                else:
+                    nc.scalar.copy(flat, banks[c, h][:])
+                nc.sync.dma_start(out=out_v[h][:, :, c * CHUNK : (c + 1) * CHUNK], in_=staged[:])
+
+        prod_tags = ["u0", "u1", "g0", "g1"]
+        pick_words(0, "w0")
+        last_product(0, prod_tags[0])
+        last_product(1, prod_tags[1])
+        for c in range(CHUNKS):
+            finish(c)
+            if c + 1 < CHUNKS:
+                pick_words(c + 1, prod_tags[c])
+            if c + 2 < CHUNKS:
+                last_product(c + 2, prod_tags[c + 2])
+            store(c)

@@ -29,7 +29,6 @@ def tile_list_products_of_two_tables_kernel(
     tc, xa, xb, fk, w_words, w_scales, xq_words, xq_scales, wq_words, wq_scales, offs, offs2, out
 ):
     nc = tc.nc
-    last = PACK - 1
     with ExitStack() as ctx:
         keep = ctx.enter_context(tc.tile_pool(name="keep", bufs=1))
         psum = ctx.enter_context(tc.psum_pool(name="psum", bufs=1))
@@ -65,59 +64,65 @@ def tile_list_products_of_two_tables_kernel(
             nc.sync.dma_start(out=b_planes[t][:], in_=xb_planes[t])
 
         nc.sync.dma_start(list_b[:], offs2)
+        for q in range(4):
+            load_scale_rows(nc.sync if q < 2 else nc.scalar, xs_table, xq_scales, q)
         load_a(0)
         nc.sync.dma_start(list_a[:], offs)
-        load_b(0)
-        for q in range(4):
-            load_scale_rows(nc.scalar, xs_table, xq_scales, q)
         load_a(1)
-        load_b(1)
         nc.sync.dma_start(out=fk_sb[:], in_=fk.rearrange("(p t) o -> p (t o)", t=PACK))
         load_a(2)
-        load_b(2)
-        for q in range(3):
+        load_b(0)
+        load_a(3)
+        for q in range(2):
+            load_scale_rows(nc.sync, wqs_sb, wq_scales, q)
+        load_b(1)
+        for q in range(2, 4):
             load_scale_rows(nc.sync, wqs_sb, wq_scales, q)
         nc.sync.dma_start(out=xq_table[:], in_=xq_words[0].rearrange("p n t -> p (n t)").bitcast(I32))
-        load_scale_rows(nc.sync, wqs_sb, wq_scales, 3)
+        nc.sync.dma_start(out=wq_sb[:].bitcast(I32), in_=wq_words[0].bitcast(I32))
+        load_b(2)
         load_scale_rows(nc.sync, ws_sb, w_scales, 0)
-        load_a(3)
         load_b(3)
         for q in range(1, 4):
             load_scale_rows(nc.sync, ws_sb, w_scales, q)
-        nc.sync.dma_start(out=wq_sb[:].bitcast(I32), in_=wq_words[0].bitcast(I32))
         nc.sync.dma_start(out=w_sb[:].bitcast(I32), in_=w_words[0].bitcast(I32))
 
         xs_picked = keep.tile([P, J], U8, name="xs_picked", align_bytes=64)
         nc.vector.tensor_copy(xs_picked[:], xs_table[:].indirect(list_b[:]))
 
-        grouped = [
-            keep.tile([P, CHUNK, PACK], BF16, name="grouped%d" % c, tag="g%d" % c, align_bytes=64)
-            for c in range(CHUNKS)
-        ]
+        grouped = keep.tile([P, J, PACK], BF16, name="grouped", align_bytes=64)
 
-        def scale_round(c, t, prod):
-            nc.scalar.activation(grouped[c][:, :, t], prod, COPY, scale=fk_sb[:, t : t + 1])
-
-        a_picked = []
-        for t in range(PACK):
-            picked = keep.tile([P, J], F32, name="a_picked%d" % t)
-            nc.vector.tensor_copy(picked[:], a_planes[t][:].indirect(list_a[:]))
-            a_picked.append(picked)
-            if t < last:
-                prod = keep.tile([P, J], F32, name="prod%d" % t)
-                nc.vector.tensor_tensor(prod[:], b_planes[t][:].indirect(list_b[:]), picked[:], MULT)
-                for c in range(CHUNKS):
-                    scale_round(c, t, prod[:, c * CHUNK : (c + 1) * CHUNK])
+        def chunk_cols(c):
+            return slice(c * CHUNK, (c + 1) * CHUNK)
 
         def chunk_list(c):
             return list_b[:, c * LIST_COLS : (c + 1) * LIST_COLS]
 
-        def last_product(c, tag):
-            prod = keep.tile([P, CHUNK], F32, name="prod_last%d" % c, tag=tag, align_bytes=64)
-            nc.vector.tensor_tensor(
-                prod[:], b_planes[last][:].indirect(chunk_list(c)), a_picked[last][:, c * CHUNK : (c + 1) * CHUNK], MULT
-            )
-            scale_round(c, last, prod[:])
+        def pick_a(t):
+            picked = keep.tile([P, J], F32, name="a_picked%d" % t)
+            nc.vector.tensor_copy(picked[:], a_planes[t][:].indirect(list_a[:]))
+            scaled = keep.tile([P, J], F32, name="a_scaled%d" % t)
+            nc.scalar.activation(scaled[:], picked[:], COPY, scale=fk_sb[:, t : t + 1])
+            return scaled
+
+        def round_pair(copy, cols, t, pair):
+            copy(grouped[:, cols, t : t + 2], pair.rearrange("p t j -> p j t"))
+
+        a_scaled = [pick_a(t) for t in range(3)]
+        low = keep.tile([P, 2, J], F32, name="low")
+        for t in range(2):
+            nc.vector.tensor_tensor(low[:, t, :], b_planes[t][:].indirect(list_b[:]), a_scaled[t][:], MULT)
+            if t == 0:
+                a_scaled.append(pick_a(3))
+        round_pair(nc.scalar.copy, slice(0, J), 0, low[:])
+
+        def high_products(c, tag):
+            high = keep.tile([P, 2, CHUNK], F32, name="high%d" % c, tag=tag, align_bytes=64)
+            for i in range(2):
+                nc.vector.tensor_tensor(
+                    high[:, i, :], b_planes[2 + i][:].indirect(chunk_list(c)), a_scaled[2 + i][:, chunk_cols(c)], MULT
+                )
+            round_pair(nc.scalar.copy if c < 2 else nc.vector.tensor_copy, chunk_cols(c), 2, high[:])
 
         banks = {}
 
@@ -137,10 +142,10 @@ def tile_list_products_of_two_tables_kernel(
                         stop=(not first and i == HALF - 1),
                     )
 
-        def pick_words(c, tag):
-            picked = keep.tile([P, CHUNK], U32, name="xq_picked%d" % c, tag=tag, align_bytes=64)
-            nc.vector.tensor_copy(picked[:], xq_table[:].bitcast(U32).indirect(chunk_list(c)))
-            passes(c, wq_sb, wqs_sb, picked[:], xs_picked[:, c * CHUNK : (c + 1) * CHUNK], True)
+        xq_picked = keep.tile([P, J], U32, name="xq_picked", align_bytes=64)
+        nc.vector.tensor_copy(xq_picked[:], xq_table[:].bitcast(U32).indirect(list_b[:]))
+        for c in range(CHUNKS):
+            passes(c, wq_sb, wqs_sb, xq_picked[:, chunk_cols(c)], xs_picked[:, chunk_cols(c)], True)
 
         out_v = out.rearrange("(h i p) j -> h p i j", h=HALF, i=HALF)
 
@@ -148,7 +153,7 @@ def tile_list_products_of_two_tables_kernel(
             codes = keep.tile([P, CHUNK], U32, name="codes%d" % c, align_bytes=64)
             scales = keep.tile([P, CHUNK], U8, name="scales%d" % c, align_bytes=64)
             nc.vector.quantize_mx(
-                out=codes[:].bitcast(FP8X4), scales=scales[:], in_=grouped[c][:].rearrange("p j t -> p (j t)")
+                out=codes[:].bitcast(FP8X4), scales=scales[:], in_=grouped[:, chunk_cols(c), :].rearrange("p j t -> p (j t)")
             )
             passes(c, w_sb, ws_sb, codes[:], scales[:], False)
 
@@ -156,20 +161,16 @@ def tile_list_products_of_two_tables_kernel(
             for h in range(HALF):
                 staged = keep.tile([P, HALF, CHUNK], F32, name="staged%d_%d" % (c, h))
                 flat = staged[:].rearrange("p i j -> p (i j)")
-                if c == CHUNKS - 1 and h == 1:
+                if c >= 2 and h == 1:
                     nc.vector.tensor_copy(flat, banks[c, h][:])
                 else:
                     nc.scalar.copy(flat, banks[c, h][:])
                 nc.sync.dma_start(out=out_v[h][:, :, c * CHUNK : (c + 1) * CHUNK], in_=staged[:])
 
-        prod_tags = ["u0", "u1", "g0", "g1"]
-        pick_words(0, "w0")
-        last_product(0, prod_tags[0])
-        last_product(1, prod_tags[1])
+        high_products(0, "h0")
+        high_products(1, "h1")
         for c in range(CHUNKS):
             finish(c)
-            if c + 1 < CHUNKS:
-                pick_words(c + 1, prod_tags[c])
             if c + 2 < CHUNKS:
-                last_product(c + 2, prod_tags[c + 2])
+                high_products(c + 2, "h%d" % c)
             store(c)

@@ -45,9 +45,9 @@ def tile_list_products_of_two_tables_kernel(
         ws_sb = keep.tile([P, N], U8, name="ws_sb", align_bytes=64)
         wqs_sb = keep.tile([P, N], U8, name="wqs_sb", align_bytes=64)
 
-        nc.gpsimd.memset(xs_table[:].bitcast(I32), 0)
-        nc.gpsimd.memset(ws_sb[:].bitcast(I32), 0)
-        nc.gpsimd.memset(wqs_sb[:].bitcast(I32), 0)
+        nc.vector.memset(xs_table[:].bitcast(I32), 0)
+        nc.vector.memset(ws_sb[:].bitcast(I32), 0)
+        nc.vector.memset(wqs_sb[:].bitcast(I32), 0)
 
         xa_planes = xa.rearrange("(p t) c -> t p c", t=PACK)
         xb_planes = xb.rearrange("(p t) c -> t p c", t=PACK)

from contextlib import ExitStack

import concourse.mybir as mybir

K, T, S, L, J, N = 512, 1024, 1024, 512, 512, 512
FLOPS = 2 * (K + L) * N * J

F32 = mybir.dt.float32
BF16 = mybir.dt.bfloat16
I32 = mybir.dt.int32
U32 = mybir.dt.uint32
U16 = mybir.dt.uint16
U8 = mybir.dt.uint8
FP8X4 = mybir.dt.float8_e4m3fn_x4
FP4X4 = mybir.dt.float4_e2m1fn_x4
MULT = mybir.AluOpType.mult
COPY = mybir.ActivationFunctionType.Copy

P = 128
PACK = 4
CHUNK = 128
CHUNKS = J // CHUNK
M_TILE = 128
HALF = 2
LIST_COLS = CHUNK // 16


def tile_list_products_of_two_tables_kernel(
    tc, xa, xb, fk, w_words, w_scales, xq_words, xq_scales, wq_words, wq_scales, offs, offs2, out
):
    nc = tc.nc
    with ExitStack() as ctx:
        keep = ctx.enter_context(tc.tile_pool(name="keep", bufs=1))
        psum = ctx.enter_context(tc.psum_pool(name="psum", bufs=1))

        list_a = keep.tile([P, J // 16], U16, name="list_a")
        list_b = keep.tile([P, J // 16], U16, name="list_b")
        a_planes = [keep.tile([P, T], F32, name="a%d" % t) for t in range(PACK)]
        b_planes = [keep.tile([P, S], F32, name="b%d" % t) for t in range(PACK)]
        fk_sb = keep.tile([P, PACK], F32, name="fk_sb")
        xq_table = keep.tile([P, S], I32, name="xq_table", align_bytes=64)
        xs_table = keep.tile([P, S], U8, name="xs_table", align_bytes=64)
        w_sb = keep.tile([P, 2 * N], U8, name="w_sb", align_bytes=64)
        wq_sb = keep.tile([P, 2 * N], U8, name="wq_sb", align_bytes=64)
        ws_sb = keep.tile([P, N], U8, name="ws_sb", align_bytes=64)
        wqs_sb = keep.tile([P, N], U8, name="wqs_sb", align_bytes=64)

        nc.vector.memset(xs_table[:].bitcast(I32), 0)
        nc.vector.memset(ws_sb[:].bitcast(I32), 0)
        nc.vector.memset(wqs_sb[:].bitcast(I32), 0)

        xa_planes = xa.rearrange("(p t) c -> t p c", t=PACK)
        xb_planes = xb.rearrange("(p t) c -> t p c", t=PACK)

        def load_scale_rows(queue, plane, scales, q):
            queue.dma_start(
                out=plane[32 * q : 32 * q + 4, :].bitcast(I32), in_=scales[0, 4 * q : 4 * q + 4, :].bitcast(I32)
            )

        def load_a(t):
            nc.sync.dma_start(out=a_planes[t][:], in_=xa_planes[t])

        def load_b(t):
            nc.sync.dma_start(out=b_planes[t][:], in_=xb_planes[t])

        nc.sync.dma_start(list_b[:], offs2)
        for q in range(4):
            load_scale_rows(nc.sync if q < 2 else nc.scalar, xs_table, xq_scales, q)
        load_a(0)
        nc.sync.dma_start(list_a[:], offs)
        load_a(1)
        nc.sync.dma_start(out=fk_sb[:], in_=fk.rearrange("(p t) o -> p (t o)", t=PACK))
        load_a(2)
        load_b(0)
        load_a(3)
        for q in range(2):
            load_scale_rows(nc.sync, wqs_sb, wq_scales, q)
        load_b(1)
        for q in range(2, 4):
            load_scale_rows(nc.sync, wqs_sb, wq_scales, q)
        nc.sync.dma_start(out=xq_table[:], in_=xq_words[0].rearrange("p n t -> p (n t)").bitcast(I32))
        nc.sync.dma_start(out=wq_sb[:].bitcast(I32), in_=wq_words[0].bitcast(I32))
        load_b(2)
        load_scale_rows(nc.sync, ws_sb, w_scales, 0)
        load_b(3)
        for q in range(1, 4):
            load_scale_rows(nc.sync, ws_sb, w_scales, q)
        nc.sync.dma_start(out=w_sb[:].bitcast(I32), in_=w_words[0].bitcast(I32))

        xs_picked = keep.tile([P, J], U8, name="xs_picked", align_bytes=64)
        nc.vector.tensor_copy(xs_picked[:], xs_table[:].indirect(list_b[:]))

        grouped = keep.tile([P, J, PACK], BF16, name="grouped", align_bytes=64)

        def chunk_cols(c):
            return slice(c * CHUNK, (c + 1) * CHUNK)

        def chunk_list(c):
            return list_b[:, c * LIST_COLS : (c + 1) * LIST_COLS]

        def pick_a(t):
            picked = keep.tile([P, J], F32, name="a_picked%d" % t)
            nc.vector.tensor_copy(picked[:], a_planes[t][:].indirect(list_a[:]))
            scaled = keep.tile([P, J], F32, name="a_scaled%d" % t)
            nc.scalar.activation(scaled[:], picked[:], COPY, scale=fk_sb[:, t : t + 1])
            return scaled

        def round_pair(copy, cols, t, pair):
            copy(grouped[:, cols, t : t + 2], pair.rearrange("p t j -> p j t"))

        a_scaled = [pick_a(t) for t in range(3)]
        low = keep.tile([P, 2, J], F32, name="low")
        for t in range(2):
            nc.vector.tensor_tensor(low[:, t, :], b_planes[t][:].indirect(list_b[:]), a_scaled[t][:], MULT)
            if t == 0:
                a_scaled.append(pick_a(3))
        round_pair(nc.scalar.copy, slice(0, J), 0, low[:])

        def high_products(c, tag):
            high = keep.tile([P, 2, CHUNK], F32, name="high%d" % c, tag=tag, align_bytes=64)
            for i in range(2):
                nc.vector.tensor_tensor(
                    high[:, i, :], b_planes[2 + i][:].indirect(chunk_list(c)), a_scaled[2 + i][:, chunk_cols(c)], MULT
                )
            round_pair(nc.scalar.copy if c < 2 else nc.vector.tensor_copy, chunk_cols(c), 2, high[:])

        banks = {}

        def passes(c, words, scales, rhs, rhs_scale, first):
            for h in range(HALF):
                if first:
                    banks[c, h] = psum.tile([P, HALF * CHUNK], F32, name="bank%d_%d" % (c, h))
                for i in range(HALF):
                    m = HALF * h + i
                    nc.tensor.matmul_mx(
                        out=banks[c, h][:, i * CHUNK : (i + 1) * CHUNK],
                        lhsT=words[:, 2 * m * M_TILE : 2 * (m + 1) * M_TILE].bitcast(FP4X4),
                        lhsT_scale=scales[:, m * M_TILE : (m + 1) * M_TILE],
                        rhs=rhs.bitcast(FP8X4),
                        rhs_scale=rhs_scale,
                        start=(first and i == 0),
                        stop=(not first and i == HALF - 1),
                    )

        xq_picked = keep.tile([P, J], U32, name="xq_picked", align_bytes=64)
        nc.vector.tensor_copy(xq_picked[:], xq_table[:].bitcast(U32).indirect(list_b[:]))
        for c in range(CHUNKS):
            passes(c, wq_sb, wqs_sb, xq_picked[:, chunk_cols(c)], xs_picked[:, chunk_cols(c)], True)

        out_v = out.rearrange("(h i p) j -> h p i j", h=HALF, i=HALF)

        def finish(c):
            codes = keep.tile([P, CHUNK], U32, name="codes%d" % c, align_bytes=64)
            scales = keep.tile([P, CHUNK], U8, name="scales%d" % c, align_bytes=64)
            nc.vector.quantize_mx(
                out=codes[:].bitcast(FP8X4), scales=scales[:], in_=grouped[:, chunk_cols(c), :].rearrange("p j t -> p (j t)")
            )
            passes(c, w_sb, ws_sb, codes[:], scales[:], False)

        def store(c):
            for h in range(HALF):
                staged = keep.tile([P, HALF, CHUNK], F32, name="staged%d_%d" % (c, h))
                flat = staged[:].rearrange("p i j -> p (i j)")
                if c >= 2 and h == 1:
                    nc.vector.tensor_copy(flat, banks[c, h][:])
                else:
                    nc.scalar.copy(flat, banks[c, h][:])
                nc.sync.dma_start(out=out_v[h][:, :, c * CHUNK : (c + 1) * CHUNK], in_=staged[:])

        high_products(0, "h0")
        high_products(1, "h1")
        for c in range(CHUNKS):
            finish(c)
            if c + 2 < CHUNKS:
                high_products(c + 2, "h%d" % c)
            store(c)
